import numpy as np
import ml_dtypes


def mxq(x, axis, fmt="e4m3"):
    dtype, down = {"e4m3": (ml_dtypes.float8_e4m3fn, 7), "e5m2": (ml_dtypes.float8_e5m2, 14)}[fmt]
    v = np.moveaxis(np.asarray(x, np.float32).astype(ml_dtypes.bfloat16).astype(np.float64), axis, -1)
    blocks = v.reshape(v.shape[:-1] + (-1, 32))
    amax = np.abs(blocks).max(-1, keepdims=True)
    byte = np.maximum(np.where(amax > 0, np.frexp(amax)[1] - 1 + 127, 0) - down, 1)
    scale = np.exp2(byte - 127.0)
    codes = (blocks / scale).astype(np.float32).astype(dtype).astype(np.float64)
    return np.moveaxis((codes * scale).reshape(v.shape), -1, axis)


WIDE = False


def mx_kscale(k):
    if not WIDE:
        return np.ones(k)
    levels = np.array([10, -10, 5, -5, 0])
    if k % 512:
        return np.exp2(np.random.permutation(np.resize(levels, k // 32))).repeat(32)
    a = np.empty((k // 512, 16))
    for p in range(k // 512):
        a[p, :8] = np.random.permutation(np.resize(levels, 8))
        for g in range(8):
            far = levels[np.abs(levels - a[p, g]) >= 10]
            a[p, g + 8] = far[np.random.randint(len(far))]
    return np.exp2(a.ravel()).repeat(32)


def f64(x):
    return np.asarray(x).astype(np.float64)


def striped(idx):
    return np.tile(idx.reshape(-1, 16).T, (8, 1)).astype(np.uint16)


def unstriped(offs):
    return offs[:16].T.reshape(-1).astype(np.int64)


def striped8(idx):
    return np.concatenate([x.reshape(-1, 16).T for x in idx]).astype(np.uint16)


def runs(offs, k):
    lists = np.stack([offs[16 * r : 16 * r + 16].T.reshape(-1) for r in range(8)]).astype(np.int64)
    return lists[np.arange(k) % 512 // 64]


def pack_weight(w):
    k, n = w.shape
    w = f64(np.asarray(w, np.float32).astype(ml_dtypes.bfloat16)).reshape(k // 32, 32, n)
    amax = np.abs(w).max(1)
    byte = np.clip(np.where(amax > 0, np.frexp(amax)[1] - 1 + 127 - 7, 1), 1, 254)
    scaled = (w * np.exp2(127.0 - byte)[:, None, :]).reshape(k, n).astype(np.float32)
    words = np.ascontiguousarray(scaled.reshape(k // 512, 128, 4, n).transpose(0, 1, 3, 2)).astype(ml_dtypes.float8_e4m3fn).view(np.uint8)
    return words, np.ascontiguousarray(byte.astype(np.uint8).reshape(k // 512, 16, n))


def unpack_weight(words, scales):
    g, p, n, _ = words.shape
    vals = np.ascontiguousarray(words).view(ml_dtypes.float8_e4m3fn).astype(np.float64) * np.repeat(np.exp2(scales.astype(np.float64) - 127.0), 8, axis=1)[..., None]
    return vals.transpose(0, 1, 3, 2).reshape(g * 512, n)


def sigmoid(v):
    return 1.0 / (1.0 + np.exp(-np.maximum(v, -700.0)))

def planes(y):
    n, m = y.shape
    v = y.astype(np.float32).astype(ml_dtypes.bfloat16).astype(np.float64).reshape(n // 32, 32, m)
    top = np.abs(v).max(1)
    byte = np.clip(np.where(top > 0, np.frexp(top)[1] - 1 + 127 - 7, 1), 1, 254)
    codes = (v * np.exp2(127.0 - byte)[:, None, :]).reshape(n, m).astype(np.float32).astype(ml_dtypes.float8_e4m3fn).view(np.uint8)
    words = codes.reshape(n // 512, 128, 4, m).transpose(0, 1, 3, 2)
    return np.ascontiguousarray(words), np.ascontiguousarray(byte.astype(np.uint8).reshape(n // 512, 16, m))


K, T, S, N, G, H = 512, 2048, 512, 512, 2048, 512


def setup_inputs():
    n = np.random.standard_normal
    s = mx_kscale(K)[:, None]
    u = mx_kscale(S)
    packed_xT = pack_weight(n((K, T)) * s)
    packed_dT = pack_weight(n((K, G)) / s)
    packed_w1 = pack_weight(n((H, N)) / np.sqrt(H) / u[:, None])
    return {
        "x_words": packed_xT[0],
        "x_scales": packed_xT[1],
        "d_words": packed_dT[0],
        "d_scales": packed_dT[1],
        "gn": (np.random.uniform(0.5, 1.5, (H, 1)) * u[:, None]).astype(np.float32),
        "w1_words": packed_w1[0],
        "w1_scales": packed_w1[1],
        "offs": striped(np.random.permutation(T)[:S]),
        "kidx": striped8(np.random.randint(0, G, (8, H))),
        "n1": striped8(np.stack([np.random.permutation(S) for _ in range(8)])),
        "n2": striped8(np.stack([np.random.permutation(S) for _ in range(8)])),
        "n3": striped8(np.stack([np.random.permutation(S) for _ in range(8)])),
    }


def reference(x_words, x_scales, d_words, d_scales, gn, w1_words, w1_scales, offs, kidx, n1, n2, n3):
    d_kidx = unpack_weight(d_words, d_scales)[np.arange(K)[:, None], runs(kidx, K)]
    xq = unpack_weight(x_words, x_scales)[:, unstriped(offs)]
    s = 0.0625 * (d_kidx.T @ xq)
    pa = s[np.arange(H)[:, None], runs(n1, H)]
    pb = s[np.arange(H)[:, None], runs(n2, H)]
    mu = 0.3125 * (s + pa + pb)
    z = f64(gn) * ((s - mu) / (np.sqrt((pa - mu) ** 2 + (pb - mu) ** 2 + 0.25)))
    h = unpack_weight(w1_words, w1_scales).T @ mxq(z, 0, "e4m3")
    out_0 = h * (sigmoid(h[np.arange(N)[:, None], runs(n3, N)]))
    return (out_0,) + planes(out_0)

@@ -1,0 +1,245 @@
+import math
+from contextlib import ExitStack
+
+import concourse.mybir as mybir
+from concourse.masks import make_identity
+
+F32 = mybir.dt.float32
+BF16 = mybir.dt.bfloat16
+I32 = mybir.dt.int32
+U32 = mybir.dt.uint32
+U16 = mybir.dt.uint16
+U8 = mybir.dt.uint8
+FP8X4 = mybir.dt.float8_e4m3fn_x4
+ALU = mybir.AluOpType
+ACT = mybir.ActivationFunctionType
+
+P = 128
+PACK = 4
+TABLE = 2048
+S = 512
+HALF = 256
+LIST_COLS = S // 16
+HALF_COLS = HALF // 16
+
+FLOPS = 2 * 2 * 512 * 512 * 512
+
+
+def tile_picked_keystdgate_none_po_kernel(
+    tc, x_words, x_scales, d_words, d_scales, gn, w1_words, w1_scales, offs, kidx, n1, n2, n3, out_0, out_1, out_2
+):
+    nc = tc.nc
+    with ExitStack() as ctx:
+        lists = ctx.enter_context(tc.tile_pool(name="lists", bufs=1))
+        keep = ctx.enter_context(tc.tile_pool(name="keep", bufs=1))
+        acc = ctx.enter_context(tc.psum_pool(name="acc", bufs=4))
+        turn = ctx.enter_context(tc.psum_pool(name="turn", bufs=2))
+
+        def words_of(dram):
+            return dram[0].rearrange("p n t -> p (n t)").bitcast(I32)
+
+        def half_cols(h):
+            return slice(h * HALF, (h + 1) * HALF)
+
+        def half_list(tile, h):
+            return tile[:, h * HALF_COLS : (h + 1) * HALF_COLS]
+
+        def sb(shape, dtype, name):
+            return keep.tile(shape, dtype, name=name, align_bytes=64)
+
+        kidx_t = lists.tile([P, LIST_COLS], U16, name="kidx_t")
+        offs_t = lists.tile([P, LIST_COLS], U16, name="offs_t")
+        n1_t = lists.tile([P, LIST_COLS], U16, name="n1_t")
+        n2_t = lists.tile([P, LIST_COLS], U16, name="n2_t")
+        n3_t = lists.tile([P, LIST_COLS], U16, name="n3_t")
+
+        d_tab = sb([P, TABLE], I32, "d_tab")
+        x_tab = sb([P, TABLE], I32, "x_tab")
+        ds_tab = sb([P, TABLE], U8, "ds_tab")
+        xs_tab = sb([P, TABLE], U8, "xs_tab")
+        w1s_raw = sb([P, S], U8, "w1s_raw")
+        gn_t = sb([P, PACK], F32, "gn_t")
+
+        quarter = sb([P, 1], F32, "quarter")
+        warm = sb([P, 1], F32, "warm")
+        nc.vector.memset(quarter[:], 0.25)
+        nc.scalar.activation(warm[:], quarter[:], ACT.Abs_reciprocal_sqrt, bias=quarter[:])
+
+        nc.sync.dma_start(kidx_t[:], kidx)
+        nc.sync.dma_start(ds_tab[:].bitcast(I32), d_scales[0].bitcast(I32).unsqueeze(1).to_broadcast([16, 8, TABLE // 4]))
+        nc.sync.dma_start(offs_t[:], offs)
+        xs_rows = x_scales[0].bitcast(I32)
+        for i in range(4):
+            nc.sync.dma_start(xs_tab[i:P:4, :].bitcast(I32), xs_rows[i:16:4, :].unsqueeze(1).to_broadcast([4, 8, TABLE // 4]))
+        nc.sync.dma_start(d_tab[:], words_of(d_words))
+        nc.sync.dma_start(x_tab[:], words_of(x_words))
+        nc.sync.dma_start(n1_t[:], n1)
+        nc.sync.dma_start(n2_t[:], n2)
+        nc.sync.dma_start(n3_t[:], n3)
+
+        ident = sb([P, P], F32, "ident")
+        make_identity(nc, ident[:])
+        nc.gpsimd.memset(w1s_raw[:].bitcast(I32), 0)
+        nc.gpsimd.dma_start(gn_t[:], gn.rearrange("(p t) o -> p (t o)", t=PACK))
+        for q in range(4):
+            nc.gpsimd.dma_start(w1s_raw[32 * q : 32 * q + 4, :].bitcast(I32), w1_scales[0, 4 * q : 4 * q + 4, :].bitcast(I32))
+
+        def deal(dst, src):
+            nc.vector.tensor_copy(dst.rearrange("p (t m) -> p m t", t=PACK), src.rearrange("p (m t) -> p m t", t=PACK))
+
+        ds_got = sb([P, S], U8, "ds_got")
+        ds_plane = sb([P, S], U8, "ds_plane")
+        nc.vector.tensor_copy(ds_got[:], ds_tab[:].indirect(kidx_t[:]))
+        deal(ds_plane[:], ds_got[:])
+        for i in range(1, 4):
+            nc.scalar.dma_start(ds_plane[i:P:32, :].bitcast(I32), ds_plane[8 * i : P : 32, :].bitcast(I32))
+
+        xs_plane = sb([P, S], U8, "xs_plane")
+        nc.vector.tensor_copy(xs_plane[:], xs_tab[:].indirect(offs_t[:]))
+        w1_raw = keep.tile([P, S], I32, name="w1_raw", tag="xs_tab", align_bytes=64)
+        nc.sync.dma_start(w1_raw[:], words_of(w1_words))
+
+        d_got = sb([P, S], U32, "d_got")
+        d_codes = sb([P, S], U32, "d_codes")
+        nc.vector.tensor_copy(d_got[:], d_tab[:].bitcast(U32).indirect(kidx_t[:]))
+        deal(d_codes[:].bitcast(I32), d_got[:].bitcast(I32))
+
+        x_codes = [sb([P, HALF], U32, f"x_codes{h}") for h in range(2)]
+        for h in range(2):
+            nc.vector.tensor_copy(x_codes[h][:], x_tab[:].bitcast(U32).indirect(half_list(offs_t, h)))
+
+        def product_pair(codes, plane, pair, rhs, rhs_plane, name):
+            ps = acc.tile([P, 2, HALF], F32, name=name, tag="acc")
+            for a in range(2):
+                rows = slice((2 * pair + a) * P, (2 * pair + a + 1) * P)
+                nc.tensor.matmul_mx(ps[:, a, :], lhsT=codes[:, rows].bitcast(FP8X4), lhsT_scale=plane[:, rows],
+                                    rhs=rhs.bitcast(FP8X4), rhs_scale=rhs_plane, start=True, stop=True)
+            return ps
+
+        raw = {}
+        for pair in range(2):
+            for h in range(2):
+                raw[h, pair] = product_pair(d_codes, ds_plane, pair, x_codes[h][:], xs_plane[:, half_cols(h)], f"s{h}{pair}")
+
+        w1_codes = sb([P, S], U32, "w1_codes")
+        w1s_plane = sb([P, S], U8, "w1s_plane")
+        gain = sb([P, PACK], F32, "gain")
+
+        score = [sb([P, S], F32, f"score{t}") for t in range(PACK)]
+        units = [(h, t) for h in range(2) for t in range(PACK)]
+        n = len(units)
+        xk = [sb([P, 2, HALF], F32, f"xk{v}") for v in range(n // 2)]
+        yk = [sb([P, 2, HALF], F32, f"yk{v}") for v in range(n // 2)]
+        g1 = [sb([P, HALF], F32, f"g1{u}") for u in range(n)]
+        nn = [sb([P, HALF], F32, f"nn{u}") for u in range(n)]
+        ee = [sb([P, HALF], F32, f"ee{u}") for u in range(n)]
+        rr = [sb([P, HALF], F32, f"rr{u}") for u in range(n)]
+        sq = [sb([P, 4, P], F32, f"sq{u}") for u in range(n)]
+        lin, den = {}, {}
+        z_rows = [sb([P, PACK, HALF], BF16, f"z_rows{h}") for h in range(2)]
+        z_in = [sb([P, HALF, PACK], BF16, f"z_in{h}") for h in range(2)]
+        z_codes = [sb([P, HALF], U32, f"z_codes{h}") for h in range(2)]
+        z_plane = [sb([P, HALF], U8, f"z_plane{h}") for h in range(2)]
+        hid = [sb([P, S], F32, f"hid{t}") for t in range(PACK)]
+
+        def window(t, h):
+            nc.scalar.copy(score[t][:, half_cols(h)], raw[h, t // 2][:, t % 2, :])
+
+        def scaled(dst, v, factor):
+            nc.scalar.activation(dst[v][:], raw[v // 2, v % 2][:], ACT.Copy, scale=factor)
+
+        def add_turned(out, a, b):
+            nc.tensor.matmul(out, a, ident[:], start=True, stop=False, is_transpose=True)
+            nc.tensor.matmul(out, b, ident[:], start=False, stop=True, is_transpose=True)
+
+        def look_up(v):
+            pair = (2 * v, 2 * v + 1)
+            for u in pair:
+                h, t = units[u]
+                nc.vector.tensor_tensor(g1[u][:], score[t][:].indirect(half_list(n1_t, h)), xk[v][:, u % 2, :], ALU.subtract)
+            for u in pair:
+                h, t = units[u]
+                nc.vector.tensor_tensor(nn[u][:], score[t][:].indirect(half_list(n2_t, h)), g1[u][:], ALU.add)
+            for u in pair:
+                nc.vector.scalar_tensor_tensor(ee[u][:], g1[u][:], 2.0, nn[u][:], ALU.mult, ALU.subtract)
+
+        def forms(u):
+            lin[u] = turn.tile([P, 4, P], F32, name=f"lin{u}", tag="lin")
+            for b in range(2):
+                cols = slice(b * P, (b + 1) * P)
+                add_turned(lin[u][:, b, :], yk[u // 2][:, u % 2, cols], nn[u][:, cols])
+            for b in range(2):
+                cols = slice(b * P, (b + 1) * P)
+                add_turned(lin[u][:, 2 + b, :], xk[u // 2][:, u % 2, cols], ee[u][:, cols])
+
+        def squares(u):
+            unit = 1.0 / (16.0 * math.sqrt(2.0))
+            nc.scalar.activation(sq[u][:, 0:2, :], lin[u][:, 0:2, :], ACT.Square, scale=0.375 * unit)
+            nc.scalar.activation(sq[u][:, 2:4, :], lin[u][:, 2:4, :], ACT.Square, scale=unit)
+            den[u] = turn.tile([P, HALF], F32, name=f"den{u}", tag="den")
+            for b in range(2):
+                add_turned(den[u][:, b * P : (b + 1) * P], sq[u][:, b, :], sq[u][:, 2 + b, :])
+
+        def root(u):
+            nc.scalar.activation(rr[u][:], den[u][:], ACT.Abs_reciprocal_sqrt, bias=quarter[:])
+
+        def weave(dst, src):
+            nc.vector.tensor_copy(dst.rearrange("p (c i) t -> p c t i", i=4), src.rearrange("p t (c i) -> p c t i", i=4))
+
+        def standardised(u):
+            h, t = units[u]
+            nc.vector.scalar_tensor_tensor(z_rows[h][:, t, :], nn[u][:], gain[:, t : t + 1], rr[u][:], ALU.mult, ALU.mult)
+            if t == PACK - 1:
+                weave(z_in[h][:], z_rows[h][:])
+                nc.vector.quantize_mx(z_codes[h][:].bitcast(FP8X4), z_plane[h][:], z_in[h][:].rearrange("p j t -> p (j t)"))
+                for pair in range(2):
+                    ps = product_pair(w1_codes, w1s_plane, pair, z_codes[h][:], z_plane[h][:], f"h{h}{pair}")
+                    copy = nc.scalar.copy if h == 0 else nc.vector.tensor_copy
+                    for a in range(2):
+                        copy(hid[2 * pair + a][:, half_cols(h)], ps[:, a, :])
+
+        window(0, 0)
+        scaled(xk, 0, 2.2)
+        window(0, 1)
+        window(1, 0)
+        window(1, 1)
+        scaled(yk, 0, 8.0 / 15.0)
+        for t in (2, 3):
+            window(t, 0)
+            window(t, 1)
+        for v in (1, 2, 3):
+            scaled(xk, v, 2.2)
+        for v in range(n // 2):
+            look_up(v)
+        deal(w1_codes[:].bitcast(I32), w1_raw[:])
+        deal(w1s_plane[:], w1s_raw[:])
+        nc.vector.tensor_scalar(gain[:], gn_t[:], -5.0 / 256.0, None, ALU.mult)
+        forms(0)
+        for k in range(n + 1):
+            if k < n:
+                if k % 2 == 1 and k + 1 < n:
+                    scaled(yk, (k + 1) // 2, 8.0 / 15.0)
+                if k + 1 < n:
+                    forms(k + 1)
+                squares(k)
+            if k >= 1:
+                root(k - 1)
+                standardised(k - 1)
+
+        out_rows = out_0.rearrange("(p t) j -> p t j", t=PACK)
+        o_codes = sb([P, S], U32, "o_codes")
+        o_plane = sb([P, S], U8, "o_plane")
+        for h in range(2):
+            res = sb([P, PACK, HALF], F32, f"res{h}")
+            o_in = sb([P, HALF, PACK], BF16, f"o_in{h}")
+            for t in range(PACK):
+                gate = sb([P, HALF], F32, f"gate{h}{t}")
+                nc.scalar.activation(gate[:], hid[t][:].indirect(half_list(n3_t, h)), ACT.Sigmoid)
+                nc.vector.tensor_tensor(res[:, t, :], hid[t][:, half_cols(h)], gate[:], ALU.mult)
+            nc.sync.dma_start(out_rows[:, :, half_cols(h)], res[:])
+            weave(o_in[:], res[:])
+            nc.vector.quantize_mx(o_codes[:, half_cols(h)].bitcast(FP8X4), o_plane[:, half_cols(h)], o_in[:].rearrange("p j t -> p (j t)"))
+            nc.sync.dma_start(words_of(out_1)[:, half_cols(h)], o_codes[:, half_cols(h)].bitcast(I32))
+        for q in range(4):
+            queue = nc.scalar if q % 2 else nc.sync
+            queue.dma_start(out_2[0, 4 * q : 4 * q + 4, :].bitcast(I32), o_plane[32 * q : 32 * q + 4, :].bitcast(I32))

@@ -32,6 +32,8 @@ def tile_picked_keystdgate_none_po_kernel(
     with ExitStack() as ctx:
         lists = ctx.enter_context(tc.tile_pool(name="lists", bufs=1))
         keep = ctx.enter_context(tc.tile_pool(name="keep", bufs=1))
+        lay = ctx.enter_context(tc.tile_pool(name="lay", bufs=1))
+        ring = ctx.enter_context(tc.tile_pool(name="ring", bufs=2))
         acc = ctx.enter_context(tc.psum_pool(name="acc", bufs=4))
         turn = ctx.enter_context(tc.psum_pool(name="turn", bufs=2))
 
@@ -47,6 +49,9 @@ def tile_picked_keystdgate_none_po_kernel(
         def sb(shape, dtype, name):
             return keep.tile(shape, dtype, name=name, align_bytes=64)
 
+        def at(offset, shape, dtype, name):
+            return lay.tile(shape, dtype, name=name, align_bytes=64, offset=offset)
+
         kidx_t = lists.tile([P, LIST_COLS], U16, name="kidx_t")
         offs_t = lists.tile([P, LIST_COLS], U16, name="offs_t")
         n1_t = lists.tile([P, LIST_COLS], U16, name="n1_t")
@@ -54,50 +59,52 @@ def tile_picked_keystdgate_none_po_kernel(
         n3_t = lists.tile([P, LIST_COLS], U16, name="n3_t")
 
         d_tab = sb([P, TABLE], I32, "d_tab")
-        x_tab = sb([P, TABLE], I32, "x_tab")
+        x_tab = at(0, [P, TABLE], I32, "x_tab")
         ds_tab = sb([P, TABLE], U8, "ds_tab")
         xs_tab = sb([P, TABLE], U8, "xs_tab")
+        w1_raw = sb([P, S], I32, "w1_raw")
         w1s_raw = sb([P, S], U8, "w1s_raw")
         gn_t = sb([P, PACK], F32, "gn_t")
 
-        quarter = sb([P, 1], F32, "quarter")
+        quarter_row = at(8192 + 3 * 2048 - 64, [P, 32], F32, "quarter_row")
+        quarter = quarter_row[:, 0:1]
         warm = sb([P, 1], F32, "warm")
-        nc.vector.memset(quarter[:], 0.25)
-        nc.scalar.activation(warm[:], quarter[:], ACT.Abs_reciprocal_sqrt, bias=quarter[:])
 
-        nc.sync.dma_start(kidx_t[:], kidx)
-        nc.sync.dma_start(ds_tab[:].bitcast(I32), d_scales[0].bitcast(I32).unsqueeze(1).to_broadcast([16, 8, TABLE // 4]))
-        nc.sync.dma_start(offs_t[:], offs)
-        xs_rows = x_scales[0].bitcast(I32)
-        for i in range(4):
-            nc.sync.dma_start(xs_tab[i:P:4, :].bitcast(I32), xs_rows[i:16:4, :].unsqueeze(1).to_broadcast([4, 8, TABLE // 4]))
+        nc.vector.memset(ds_tab[:].bitcast(I32), 0)
+        nc.vector.memset(xs_tab[:, : TABLE // 2].bitcast(I32), 0)
+        nc.gpsimd.memset(xs_tab[:, TABLE // 2 :].bitcast(I32), 0)
+        nc.vector.memset(quarter_row[:], 0.25)
+        nc.scalar.activation(warm[:], quarter, ACT.Abs_reciprocal_sqrt, bias=quarter)
+
+        for tile, dram in ((kidx_t, kidx), (offs_t, offs), (n1_t, n1), (n2_t, n2), (n3_t, n3)):
+            nc.sync.dma_start(tile[:], dram)
+        nc.sync.dma_start(ds_tab[0:P:8, :].bitcast(I32), d_scales[0].bitcast(I32))
+        nc.sync.dma_start(xs_tab[0:P:8, :].bitcast(I32), x_scales[0].bitcast(I32))
         nc.sync.dma_start(d_tab[:], words_of(d_words))
         nc.sync.dma_start(x_tab[:], words_of(x_words))
-        nc.sync.dma_start(n1_t[:], n1)
-        nc.sync.dma_start(n2_t[:], n2)
-        nc.sync.dma_start(n3_t[:], n3)
+        nc.sync.dma_start(w1_raw[:], words_of(w1_words))
 
-        ident = sb([P, P], F32, "ident")
-        make_identity(nc, ident[:])
         nc.gpsimd.memset(w1s_raw[:].bitcast(I32), 0)
-        nc.gpsimd.dma_start(gn_t[:], gn.rearrange("(p t) o -> p (t o)", t=PACK))
         for q in range(4):
             nc.gpsimd.dma_start(w1s_raw[32 * q : 32 * q + 4, :].bitcast(I32), w1_scales[0, 4 * q : 4 * q + 4, :].bitcast(I32))
+        nc.gpsimd.dma_start(gn_t[:], gn.rearrange("(p t) o -> p (t o)", t=PACK))
+        ident = sb([P, P], F32, "ident")
+        make_identity(nc, ident[:])
 
         def deal(dst, src):
             nc.vector.tensor_copy(dst.rearrange("p (t m) -> p m t", t=PACK), src.rearrange("p (m t) -> p m t", t=PACK))
 
         ds_got = sb([P, S], U8, "ds_got")
-        ds_plane = sb([P, S], U8, "ds_plane")
+        xs_got = sb([P, S], U8, "xs_got")
+        planes = sb([P, 2 * S], U8, "planes")
+        ds_plane = planes[:, :S]
+        xs_plane = planes[:, S:]
         nc.vector.tensor_copy(ds_got[:], ds_tab[:].indirect(kidx_t[:]))
-        deal(ds_plane[:], ds_got[:])
+        nc.vector.tensor_copy(xs_got[:], xs_tab[:].indirect(offs_t[:]))
+        deal(ds_plane, ds_got[:])
+        nc.vector.tensor_copy(xs_plane.bitcast(I32), xs_got[:].bitcast(I32))
         for i in range(1, 4):
-            nc.scalar.dma_start(ds_plane[i:P:32, :].bitcast(I32), ds_plane[8 * i : P : 32, :].bitcast(I32))
-
-        xs_plane = sb([P, S], U8, "xs_plane")
-        nc.vector.tensor_copy(xs_plane[:], xs_tab[:].indirect(offs_t[:]))
-        w1_raw = keep.tile([P, S], I32, name="w1_raw", tag="xs_tab", align_bytes=64)
-        nc.sync.dma_start(w1_raw[:], words_of(w1_words))
+            nc.scalar.dma_start(planes[i:P:32, :].bitcast(I32), planes[8 * i : P : 32, :].bitcast(I32))
 
         d_got = sb([P, S], U32, "d_got")
         d_codes = sb([P, S], U32, "d_codes")
@@ -108,45 +115,44 @@ def tile_picked_keystdgate_none_po_kernel(
         for h in range(2):
             nc.vector.tensor_copy(x_codes[h][:], x_tab[:].bitcast(U32).indirect(half_list(offs_t, h)))
 
-        def product_pair(codes, plane, pair, rhs, rhs_plane, name):
-            ps = acc.tile([P, 2, HALF], F32, name=name, tag="acc")
+        def product_pair(ps, codes, plane, pair, rhs, rhs_plane):
             for a in range(2):
                 rows = slice((2 * pair + a) * P, (2 * pair + a + 1) * P)
                 nc.tensor.matmul_mx(ps[:, a, :], lhsT=codes[:, rows].bitcast(FP8X4), lhsT_scale=plane[:, rows],
                                     rhs=rhs.bitcast(FP8X4), rhs_scale=rhs_plane, start=True, stop=True)
-            return ps
 
         raw = {}
         for pair in range(2):
             for h in range(2):
-                raw[h, pair] = product_pair(d_codes, ds_plane, pair, x_codes[h][:], xs_plane[:, half_cols(h)], f"s{h}{pair}")
+                raw[h, pair] = acc.tile([P, 2, HALF], F32, name=f"s{h}{pair}", tag="acc")
+                product_pair(raw[h, pair][:], d_codes, ds_plane, pair, x_codes[h][:], xs_plane[:, half_cols(h)])
 
-        w1_codes = sb([P, S], U32, "w1_codes")
-        w1s_plane = sb([P, S], U8, "w1s_plane")
-        gain = sb([P, PACK], F32, "gain")
+        w1_codes = at(0, [P, S], U32, "w1_codes")
+        w1s_plane = at(2048, [P, S], U8, "w1s_plane")
+        gain = at(2560, [P, PACK], F32, "gain")
 
         score = [sb([P, S], F32, f"score{t}") for t in range(PACK)]
         units = [(h, t) for h in range(2) for t in range(PACK)]
         n = len(units)
+        direct = n - 1
         xk = [sb([P, 2, HALF], F32, f"xk{v}") for v in range(n // 2)]
         yk = [sb([P, 2, HALF], F32, f"yk{v}") for v in range(n // 2)]
         g1 = [sb([P, HALF], F32, f"g1{u}") for u in range(n)]
         nn = [sb([P, HALF], F32, f"nn{u}") for u in range(n)]
         ee = [sb([P, HALF], F32, f"ee{u}") for u in range(n)]
         rr = [sb([P, HALF], F32, f"rr{u}") for u in range(n)]
-        sq = [sb([P, 4, P], F32, f"sq{u}") for u in range(n)]
-        lin, den = {}, {}
+        lin, den, sq = {}, {}, {}
         z_rows = [sb([P, PACK, HALF], BF16, f"z_rows{h}") for h in range(2)]
         z_in = [sb([P, HALF, PACK], BF16, f"z_in{h}") for h in range(2)]
         z_codes = [sb([P, HALF], U32, f"z_codes{h}") for h in range(2)]
         z_plane = [sb([P, HALF], U8, f"z_plane{h}") for h in range(2)]
-        hid = [sb([P, S], F32, f"hid{t}") for t in range(PACK)]
+        hid = [at(8192 + 2048 * t, [P, S], F32, f"hid{t}") for t in range(PACK)]
 
-        def window(t, h):
-            nc.scalar.copy(score[t][:, half_cols(h)], raw[h, t // 2][:, t % 2, :])
+        def window(t, h, copy):
+            copy(score[t][:, half_cols(h)], raw[h, t // 2][:, t % 2, :])
 
-        def scaled(dst, v, factor):
-            nc.scalar.activation(dst[v][:], raw[v // 2, v % 2][:], ACT.Copy, scale=factor)
+        def scaled(dst, v, factor, count=2):
+            nc.scalar.activation(dst[v][:, :count, :], raw[v // 2, v % 2][:, :count, :], ACT.Copy, scale=factor)
 
         def add_turned(out, a, b):
             nc.tensor.matmul(out, a, ident[:], start=True, stop=False, is_transpose=True)
@@ -164,6 +170,11 @@ def tile_picked_keystdgate_none_po_kernel(
                 nc.vector.scalar_tensor_tensor(ee[u][:], g1[u][:], 2.0, nn[u][:], ALU.mult, ALU.subtract)
 
         def forms(u):
+            if u >= direct:
+                lin[u] = sb([P, 4, P], F32, f"lin_last{u}")
+                nc.vector.scalar_tensor_tensor(lin[u][:, 0:2, :].rearrange("p b c -> p (b c)"), raw[1, 1][:, u % 2, :], 8.0 / 15.0, nn[u][:], ALU.mult, ALU.add)
+                nc.vector.tensor_tensor(lin[u][:, 2:4, :].rearrange("p b c -> p (b c)"), xk[u // 2][:, u % 2, :], ee[u][:], ALU.add)
+                return
             lin[u] = turn.tile([P, 4, P], F32, name=f"lin{u}", tag="lin")
             for b in range(2):
                 cols = slice(b * P, (b + 1) * P)
@@ -174,72 +185,95 @@ def tile_picked_keystdgate_none_po_kernel(
 
         def squares(u):
             unit = 1.0 / (16.0 * math.sqrt(2.0))
+            sq[u] = ring.tile([P, 4, P], F32, name=f"sq{u}", tag="sq")
             nc.scalar.activation(sq[u][:, 0:2, :], lin[u][:, 0:2, :], ACT.Square, scale=0.375 * unit)
             nc.scalar.activation(sq[u][:, 2:4, :], lin[u][:, 2:4, :], ACT.Square, scale=unit)
+            if u >= direct:
+                den[u] = at(8192 + 1536, [P, HALF], F32, f"den_last{u}")
+                nc.vector.tensor_tensor(den[u][:], sq[u][:, 0:2, :].rearrange("p b c -> p (b c)"), sq[u][:, 2:4, :].rearrange("p b c -> p (b c)"), ALU.add)
+                return
             den[u] = turn.tile([P, HALF], F32, name=f"den{u}", tag="den")
             for b in range(2):
                 add_turned(den[u][:, b * P : (b + 1) * P], sq[u][:, b, :], sq[u][:, 2 + b, :])
 
         def root(u):
-            nc.scalar.activation(rr[u][:], den[u][:], ACT.Abs_reciprocal_sqrt, bias=quarter[:])
+            nc.scalar.activation(rr[u][:], den[u][:], ACT.Abs_reciprocal_sqrt, bias=quarter)
 
-        def weave(dst, src):
-            nc.vector.tensor_copy(dst.rearrange("p (c i) t -> p c t i", i=4), src.rearrange("p t (c i) -> p c t i", i=4))
+        def weave(copy, dst, src):
+            copy(dst.rearrange("p (c i) t -> p c t i", i=4), src.rearrange("p t (c i) -> p c t i", i=4))
 
         def standardised(u):
             h, t = units[u]
             nc.vector.scalar_tensor_tensor(z_rows[h][:, t, :], nn[u][:], gain[:, t : t + 1], rr[u][:], ALU.mult, ALU.mult)
-            if t == PACK - 1:
-                weave(z_in[h][:], z_rows[h][:])
-                nc.vector.quantize_mx(z_codes[h][:].bitcast(FP8X4), z_plane[h][:], z_in[h][:].rearrange("p j t -> p (j t)"))
-                for pair in range(2):
-                    ps = product_pair(w1_codes, w1s_plane, pair, z_codes[h][:], z_plane[h][:], f"h{h}{pair}")
-                    copy = nc.scalar.copy if h == 0 else nc.vector.tensor_copy
-                    for a in range(2):
-                        copy(hid[2 * pair + a][:, half_cols(h)], ps[:, a, :])
 
-        window(0, 0)
+        sums = {}
+        late = []
+
+        def values(h):
+            pieces = [slice(0, HALF)] if h == 0 else [slice(0, P), slice(P, HALF)]
+            for cols in pieces:
+                weave(nc.vector.tensor_copy, z_in[h][:, cols, :], z_rows[h][:, :, cols])
+            for cols in pieces:
+                nc.vector.quantize_mx(z_codes[h][:, cols].bitcast(FP8X4), z_plane[h][:, cols], z_in[h][:, cols, :].rearrange("p j t -> p (j t)"))
+            for pair in range(2):
+                sums[h, pair] = acc.tile([P, 2, HALF], F32, name=f"h{h}{pair}", tag="acc")
+            for cols in pieces:
+                for pair in range(2):
+                    product_pair(sums[h, pair][:, :, cols], w1_codes, w1s_plane, pair, z_codes[h][:, cols], z_plane[h][:, cols])
+            for t in range(PACK):
+                copy = nc.scalar.copy if h == 0 else nc.vector.tensor_copy
+                late.append((copy, t, h))
+
+        deal(w1_codes[:].bitcast(I32), w1_raw[:])
+        deal(w1s_plane[:], w1s_raw[:])
+        nc.vector.tensor_scalar(gain[:], gn_t[:], -5.0 / 256.0, None, ALU.mult)
+        for t in (0, 1):
+            window(t, 0, nc.scalar.copy)
+            window(t, 1, nc.vector.tensor_copy)
         scaled(xk, 0, 2.2)
-        window(0, 1)
-        window(1, 0)
-        window(1, 1)
         scaled(yk, 0, 8.0 / 15.0)
         for t in (2, 3):
-            window(t, 0)
-            window(t, 1)
+            window(t, 0, nc.scalar.copy)
+            window(t, 1, nc.scalar.copy)
         for v in (1, 2, 3):
             scaled(xk, v, 2.2)
         for v in range(n // 2):
             look_up(v)
-        deal(w1_codes[:].bitcast(I32), w1_raw[:])
-        deal(w1s_plane[:], w1s_raw[:])
-        nc.vector.tensor_scalar(gain[:], gn_t[:], -5.0 / 256.0, None, ALU.mult)
         forms(0)
         for k in range(n + 1):
             if k < n:
-                if k % 2 == 1 and k + 1 < n:
-                    scaled(yk, (k + 1) // 2, 8.0 / 15.0)
+                if k % 2 == 1 and k + 1 < direct:
+                    scaled(yk, (k + 1) // 2, 8.0 / 15.0, min(2, direct - k - 1))
                 if k + 1 < n:
                     forms(k + 1)
                 squares(k)
             if k >= 1:
                 root(k - 1)
                 standardised(k - 1)
+                if k % PACK == 0:
+                    values(k // PACK - 1)
+        warm_gate = sb([P, 1], F32, "warm_gate")
+        nc.scalar.activation(warm_gate[:], rr[n - 1][:, 0:1], ACT.Sigmoid)
+        for copy, t, h in late:
+            copy(hid[t][:, half_cols(h)], sums[h, t // 2][:, t % 2, :])
 
         out_rows = out_0.rearrange("(p t) j -> p t j", t=PACK)
         o_codes = sb([P, S], U32, "o_codes")
         o_plane = sb([P, S], U8, "o_plane")
-        for h in range(2):
-            res = sb([P, PACK, HALF], F32, f"res{h}")
-            o_in = sb([P, HALF, PACK], BF16, f"o_in{h}")
-            for t in range(PACK):
-                gate = sb([P, HALF], F32, f"gate{h}{t}")
-                nc.scalar.activation(gate[:], hid[t][:].indirect(half_list(n3_t, h)), ACT.Sigmoid)
-                nc.vector.tensor_tensor(res[:, t, :], hid[t][:, half_cols(h)], gate[:], ALU.mult)
-            nc.sync.dma_start(out_rows[:, :, half_cols(h)], res[:])
-            weave(o_in[:], res[:])
-            nc.vector.quantize_mx(o_codes[:, half_cols(h)].bitcast(FP8X4), o_plane[:, half_cols(h)], o_in[:].rearrange("p j t -> p (j t)"))
-            nc.sync.dma_start(words_of(out_1)[:, half_cols(h)], o_codes[:, half_cols(h)].bitcast(I32))
+        for lo, width in ((0, 256), (256, 128), (384, 128)):
+            cols = slice(lo, lo + width)
+            res = sb([P, PACK, width], F32, f"res{lo}")
+            o_in = sb([P, width, PACK], BF16, f"o_in{lo}")
+            for pair in range(2):
+                gate = sb([P, 2, width], F32, f"gate{lo}{pair}")
+                for a in range(2):
+                    nc.scalar.activation(gate[:, a, :], hid[2 * pair + a][:].indirect(n3_t[:, lo // 16 : (lo + width) // 16]), ACT.Sigmoid)
+                own = sums[lo // HALF, pair][:, :, lo % HALF : lo % HALF + width]
+                nc.vector.tensor_tensor(res[:, 2 * pair : 2 * pair + 2, :], own, gate[:], ALU.mult)
+            nc.sync.dma_start(out_rows[:, :, cols], res[:])
+            weave(nc.vector.tensor_copy, o_in[:], res[:])
+            nc.vector.quantize_mx(o_codes[:, cols].bitcast(FP8X4), o_plane[:, cols], o_in[:].rearrange("p j t -> p (j t)"))
+            nc.sync.dma_start(words_of(out_1)[:, cols], o_codes[:, cols].bitcast(I32))
         for q in range(4):
             queue = nc.scalar if q % 2 else nc.sync
             queue.dma_start(out_2[0, 4 * q : 4 * q + 4, :].bitcast(I32), o_plane[32 * q : 32 * q + 4, :].bitcast(I32))

@@ -66,7 +66,7 @@ def tile_picked_keystdgate_none_po_kernel(
         w1s_raw = sb([P, S], U8, "w1s_raw")
         gn_t = sb([P, PACK], F32, "gn_t")
 
-        quarter_row = at(8192 + 3 * 2048 - 64, [P, 32], F32, "quarter_row")
+        quarter_row = sb([P, 1], F32, "quarter_row")
         quarter = quarter_row[:, 0:1]
         warm = sb([P, 1], F32, "warm")
 
@@ -76,23 +76,27 @@ def tile_picked_keystdgate_none_po_kernel(
         nc.vector.memset(quarter_row[:], 0.25)
         nc.scalar.activation(warm[:], quarter, ACT.Abs_reciprocal_sqrt, bias=quarter)
 
-        for tile, dram in ((kidx_t, kidx), (offs_t, offs), (n1_t, n1), (n2_t, n2), (n3_t, n3)):
+        for tile, dram in ((kidx_t, kidx), (offs_t, offs), (n1_t, n1), (n2_t, n2)):
             nc.sync.dma_start(tile[:], dram)
+        nc.sync.dma_start(gn_t[:], gn.rearrange("(p t) o -> p (t o)", t=PACK))
         nc.sync.dma_start(ds_tab[0:P:8, :].bitcast(I32), d_scales[0].bitcast(I32))
         nc.sync.dma_start(xs_tab[0:P:8, :].bitcast(I32), x_scales[0].bitcast(I32))
         nc.sync.dma_start(d_tab[:], words_of(d_words))
         nc.sync.dma_start(x_tab[:], words_of(x_words))
         nc.sync.dma_start(w1_raw[:], words_of(w1_words))
 
+        nc.sync.dma_start(n3_t[:], n3)
         nc.gpsimd.memset(w1s_raw[:].bitcast(I32), 0)
-        for q in range(4):
-            nc.gpsimd.dma_start(w1s_raw[32 * q : 32 * q + 4, :].bitcast(I32), w1_scales[0, 4 * q : 4 * q + 4, :].bitcast(I32))
-        nc.gpsimd.dma_start(gn_t[:], gn.rearrange("(p t) o -> p (t o)", t=PACK))
+        nc.sync.dma_start(w1s_raw[0:P:8, :].bitcast(I32), w1_scales[0].bitcast(I32))
         ident = sb([P, P], F32, "ident")
         make_identity(nc, ident[:])
 
         def deal(dst, src):
             nc.vector.tensor_copy(dst.rearrange("p (t m) -> p m t", t=PACK), src.rearrange("p (m t) -> p m t", t=PACK))
+
+        def settle(queue, plane):
+            for i in range(1, 4):
+                queue.dma_start(plane[i:P:32, :].bitcast(I32), plane[8 * i : P : 32, :].bitcast(I32))
 
         ds_got = sb([P, S], U8, "ds_got")
         xs_got = sb([P, S], U8, "xs_got")
@@ -103,8 +107,7 @@ def tile_picked_keystdgate_none_po_kernel(
         nc.vector.tensor_copy(xs_got[:], xs_tab[:].indirect(offs_t[:]))
         deal(ds_plane, ds_got[:])
         nc.vector.tensor_copy(xs_plane.bitcast(I32), xs_got[:].bitcast(I32))
-        for i in range(1, 4):
-            nc.scalar.dma_start(planes[i:P:32, :].bitcast(I32), planes[8 * i : P : 32, :].bitcast(I32))
+        settle(nc.scalar, planes)
 
         d_got = sb([P, S], U32, "d_got")
         d_codes = sb([P, S], U32, "d_codes")
@@ -134,7 +137,7 @@ def tile_picked_keystdgate_none_po_kernel(
         score = [sb([P, S], F32, f"score{t}") for t in range(PACK)]
         units = [(h, t) for h in range(2) for t in range(PACK)]
         n = len(units)
-        direct = n - 1
+        direct = n - 2
         xk = [sb([P, 2, HALF], F32, f"xk{v}") for v in range(n // 2)]
         yk = [sb([P, 2, HALF], F32, f"yk{v}") for v in range(n // 2)]
         g1 = [sb([P, HALF], F32, f"g1{u}") for u in range(n)]
@@ -189,7 +192,7 @@ def tile_picked_keystdgate_none_po_kernel(
             nc.scalar.activation(sq[u][:, 0:2, :], lin[u][:, 0:2, :], ACT.Square, scale=0.375 * unit)
             nc.scalar.activation(sq[u][:, 2:4, :], lin[u][:, 2:4, :], ACT.Square, scale=unit)
             if u >= direct:
-                den[u] = at(8192 + 1536, [P, HALF], F32, f"den_last{u}")
+                den[u] = at(8192 + 1536, [P, HALF], F32, f"den_last{u}") if u == n - 1 else sb([P, HALF], F32, f"den_last{u}")
                 nc.vector.tensor_tensor(den[u][:], sq[u][:, 0:2, :].rearrange("p b c -> p (b c)"), sq[u][:, 2:4, :].rearrange("p b c -> p (b c)"), ALU.add)
                 return
             den[u] = turn.tile([P, HALF], F32, name=f"den{u}", tag="den")
@@ -221,16 +224,17 @@ def tile_picked_keystdgate_none_po_kernel(
                 for pair in range(2):
                     product_pair(sums[h, pair][:, :, cols], w1_codes, w1s_plane, pair, z_codes[h][:, cols], z_plane[h][:, cols])
             for t in range(PACK):
-                copy = nc.scalar.copy if h == 0 else nc.vector.tensor_copy
+                copy = nc.scalar.copy if h == 0 and t < 2 else nc.vector.tensor_copy
                 late.append((copy, t, h))
 
         deal(w1_codes[:].bitcast(I32), w1_raw[:])
         deal(w1s_plane[:], w1s_raw[:])
+        settle(nc.sync, w1s_plane)
         nc.vector.tensor_scalar(gain[:], gn_t[:], -5.0 / 256.0, None, ALU.mult)
+        scaled(xk, 0, 2.2)
         for t in (0, 1):
             window(t, 0, nc.scalar.copy)
             window(t, 1, nc.vector.tensor_copy)
-        scaled(xk, 0, 2.2)
         scaled(yk, 0, 8.0 / 15.0)
         for t in (2, 3):
             window(t, 0, nc.scalar.copy)

@@ -16,11 +16,21 @@ ACT = mybir.ActivationFunctionType
 
 P = 128
 PACK = 4
+BLOCK_PARTS = 8
+QUAD = 32
+GROUP = 16
 TABLE = 2048
 S = 512
-HALF = 256
-LIST_COLS = S // 16
-HALF_COLS = HALF // 16
+HALF = S // 2
+UNITS = [(h, t) for h in range(2) for t in range(PACK)]
+TURNED = len(UNITS) - 2
+OUT_PIECES = ((0, 256), (256, 128), (384, 128))
+
+LEAD = 11.0 / 5.0
+EVEN = 8.0 / 15.0
+ODD_SCALE = 1.0 / math.sqrt(512.0)
+EVEN_SCALE = 0.375 * ODD_SCALE
+GAIN = -5.0 / 256.0
 
 FLOPS = 2 * 2 * 512 * 512 * 512
 
@@ -32,10 +42,19 @@ def tile_picked_keystdgate_none_po_kernel(
     with ExitStack() as ctx:
         lists = ctx.enter_context(tc.tile_pool(name="lists", bufs=1))
         keep = ctx.enter_context(tc.tile_pool(name="keep", bufs=1))
-        lay = ctx.enter_context(tc.tile_pool(name="lay", bufs=1))
+        reused = ctx.enter_context(tc.tile_pool(name="reused", bufs=1))
         ring = ctx.enter_context(tc.tile_pool(name="ring", bufs=2))
-        acc = ctx.enter_context(tc.psum_pool(name="acc", bufs=4))
-        turn = ctx.enter_context(tc.psum_pool(name="turn", bufs=2))
+        products = ctx.enter_context(tc.psum_pool(name="products", bufs=4))
+        turns = ctx.enter_context(tc.psum_pool(name="turns", bufs=2))
+
+        def sb(shape, dtype, name):
+            return keep.tile(shape, dtype, name=name, align_bytes=64)
+
+        def on_x_table(offset, shape, dtype, name):
+            return reused.tile(shape, dtype, name=name, align_bytes=64, offset=offset)
+
+        def in_ring(shape, dtype, name):
+            return ring.tile(shape, dtype, name=name, tag="ring", align_bytes=64)
 
         def words_of(dram):
             return dram[0].rearrange("p n t -> p (n t)").bitcast(I32)
@@ -43,51 +62,45 @@ def tile_picked_keystdgate_none_po_kernel(
         def half_cols(h):
             return slice(h * HALF, (h + 1) * HALF)
 
-        def half_list(tile, h):
-            return tile[:, h * HALF_COLS : (h + 1) * HALF_COLS]
+        def entries(list_tile, lo, count):
+            return list_tile[:, lo // GROUP : (lo + count) // GROUP]
 
-        def sb(shape, dtype, name):
-            return keep.tile(shape, dtype, name=name, align_bytes=64)
+        def flat(ap):
+            return ap.rearrange("p b c -> p (b c)")
 
-        def at(offset, shape, dtype, name):
-            return lay.tile(shape, dtype, name=name, align_bytes=64, offset=offset)
+        kidx_t = lists.tile([P, S // GROUP], U16, name="kidx_t")
+        offs_t = lists.tile([P, S // GROUP], U16, name="offs_t")
+        n1_t = lists.tile([P, S // GROUP], U16, name="n1_t")
+        n2_t = lists.tile([P, S // GROUP], U16, name="n2_t")
+        n3_t = lists.tile([P, S // GROUP], U16, name="n3_t")
 
-        kidx_t = lists.tile([P, LIST_COLS], U16, name="kidx_t")
-        offs_t = lists.tile([P, LIST_COLS], U16, name="offs_t")
-        n1_t = lists.tile([P, LIST_COLS], U16, name="n1_t")
-        n2_t = lists.tile([P, LIST_COLS], U16, name="n2_t")
-        n3_t = lists.tile([P, LIST_COLS], U16, name="n3_t")
-
-        d_tab = sb([P, TABLE], I32, "d_tab")
-        x_tab = at(0, [P, TABLE], I32, "x_tab")
-        ds_tab = sb([P, TABLE], U8, "ds_tab")
-        xs_tab = sb([P, TABLE], U8, "xs_tab")
-        w1_raw = sb([P, S], I32, "w1_raw")
-        w1s_raw = sb([P, S], U8, "w1s_raw")
+        d_table = sb([P, TABLE], I32, "d_table")
+        x_table = on_x_table(0, [P, TABLE], I32, "x_table")
+        d_scale_table = sb([P, TABLE], U8, "d_scale_table")
+        x_scale_table = sb([P, TABLE], U8, "x_scale_table")
+        w1_loaded = sb([P, S], I32, "w1_loaded")
+        w1_scale_loaded = sb([P, S], U8, "w1_scale_loaded")
         gn_t = sb([P, PACK], F32, "gn_t")
+        quarter = sb([P, 1], F32, "quarter")
+        warm_root = sb([P, 1], F32, "warm_root")
 
-        quarter_row = sb([P, 1], F32, "quarter_row")
-        quarter = quarter_row[:, 0:1]
-        warm = sb([P, 1], F32, "warm")
+        nc.vector.memset(d_scale_table[:].bitcast(I32), 0)
+        nc.vector.memset(x_scale_table[:, : TABLE // 2].bitcast(I32), 0)
+        nc.gpsimd.memset(x_scale_table[:, TABLE // 2 :].bitcast(I32), 0)
+        nc.vector.memset(quarter[:], 0.25)
+        nc.scalar.activation(warm_root[:], quarter[:], ACT.Abs_reciprocal_sqrt, bias=quarter[:])
 
-        nc.vector.memset(ds_tab[:].bitcast(I32), 0)
-        nc.vector.memset(xs_tab[:, : TABLE // 2].bitcast(I32), 0)
-        nc.gpsimd.memset(xs_tab[:, TABLE // 2 :].bitcast(I32), 0)
-        nc.vector.memset(quarter_row[:], 0.25)
-        nc.scalar.activation(warm[:], quarter, ACT.Abs_reciprocal_sqrt, bias=quarter)
-
-        for tile, dram in ((kidx_t, kidx), (offs_t, offs), (n1_t, n1), (n2_t, n2)):
-            nc.sync.dma_start(tile[:], dram)
+        for list_tile, dram in ((kidx_t, kidx), (offs_t, offs), (n1_t, n1), (n2_t, n2)):
+            nc.sync.dma_start(list_tile[:], dram)
         nc.sync.dma_start(gn_t[:], gn.rearrange("(p t) o -> p (t o)", t=PACK))
-        nc.sync.dma_start(ds_tab[0:P:8, :].bitcast(I32), d_scales[0].bitcast(I32))
-        nc.sync.dma_start(xs_tab[0:P:8, :].bitcast(I32), x_scales[0].bitcast(I32))
-        nc.sync.dma_start(d_tab[:], words_of(d_words))
-        nc.sync.dma_start(x_tab[:], words_of(x_words))
-        nc.sync.dma_start(w1_raw[:], words_of(w1_words))
-
+        nc.sync.dma_start(d_scale_table[0:P:BLOCK_PARTS, :].bitcast(I32), d_scales[0].bitcast(I32))
+        nc.sync.dma_start(x_scale_table[0:P:BLOCK_PARTS, :].bitcast(I32), x_scales[0].bitcast(I32))
+        nc.sync.dma_start(d_table[:], words_of(d_words))
+        nc.sync.dma_start(x_table[:], words_of(x_words))
+        nc.sync.dma_start(w1_loaded[:], words_of(w1_words))
         nc.sync.dma_start(n3_t[:], n3)
-        nc.gpsimd.memset(w1s_raw[:].bitcast(I32), 0)
-        nc.sync.dma_start(w1s_raw[0:P:8, :].bitcast(I32), w1_scales[0].bitcast(I32))
+        nc.gpsimd.memset(w1_scale_loaded[:].bitcast(I32), 0)
+        nc.sync.dma_start(w1_scale_loaded[0:P:BLOCK_PARTS, :].bitcast(I32), w1_scales[0].bitcast(I32))
         ident = sb([P, P], F32, "ident")
         make_identity(nc, ident[:])
 
@@ -95,189 +108,207 @@ def tile_picked_keystdgate_none_po_kernel(
             nc.vector.tensor_copy(dst.rearrange("p (t m) -> p m t", t=PACK), src.rearrange("p (m t) -> p m t", t=PACK))
 
         def settle(queue, plane):
-            for i in range(1, 4):
-                queue.dma_start(plane[i:P:32, :].bitcast(I32), plane[8 * i : P : 32, :].bitcast(I32))
+            for i in range(1, PACK):
+                queue.dma_start(plane[i:P:QUAD, :].bitcast(I32), plane[BLOCK_PARTS * i : P : QUAD, :].bitcast(I32))
 
-        ds_got = sb([P, S], U8, "ds_got")
-        xs_got = sb([P, S], U8, "xs_got")
+        d_scale_picked = sb([P, S], U8, "d_scale_picked")
+        x_scale_picked = sb([P, S], U8, "x_scale_picked")
         planes = sb([P, 2 * S], U8, "planes")
-        ds_plane = planes[:, :S]
-        xs_plane = planes[:, S:]
-        nc.vector.tensor_copy(ds_got[:], ds_tab[:].indirect(kidx_t[:]))
-        nc.vector.tensor_copy(xs_got[:], xs_tab[:].indirect(offs_t[:]))
-        deal(ds_plane, ds_got[:])
-        nc.vector.tensor_copy(xs_plane.bitcast(I32), xs_got[:].bitcast(I32))
+        d_plane = planes[:, :S]
+        x_plane = planes[:, S:]
+        nc.vector.tensor_copy(d_scale_picked[:], d_scale_table[:].indirect(kidx_t[:]))
+        nc.vector.tensor_copy(x_scale_picked[:], x_scale_table[:].indirect(offs_t[:]))
+        deal(d_plane, d_scale_picked[:])
+        nc.vector.tensor_copy(x_plane.bitcast(I32), x_scale_picked[:].bitcast(I32))
         settle(nc.scalar, planes)
 
-        d_got = sb([P, S], U32, "d_got")
+        d_picked = sb([P, S], U32, "d_picked")
         d_codes = sb([P, S], U32, "d_codes")
-        nc.vector.tensor_copy(d_got[:], d_tab[:].bitcast(U32).indirect(kidx_t[:]))
-        deal(d_codes[:].bitcast(I32), d_got[:].bitcast(I32))
-
+        nc.vector.tensor_copy(d_picked[:], d_table[:].bitcast(U32).indirect(kidx_t[:]))
+        deal(d_codes[:].bitcast(I32), d_picked[:].bitcast(I32))
         x_codes = [sb([P, HALF], U32, f"x_codes{h}") for h in range(2)]
         for h in range(2):
-            nc.vector.tensor_copy(x_codes[h][:], x_tab[:].bitcast(U32).indirect(half_list(offs_t, h)))
+            nc.vector.tensor_copy(x_codes[h][:], x_table[:].bitcast(U32).indirect(entries(offs_t, h * HALF, HALF)))
 
-        def product_pair(ps, codes, plane, pair, rhs, rhs_plane):
+        def product_pair(bank, codes, plane, pair, rhs, rhs_plane):
             for a in range(2):
                 rows = slice((2 * pair + a) * P, (2 * pair + a + 1) * P)
-                nc.tensor.matmul_mx(ps[:, a, :], lhsT=codes[:, rows].bitcast(FP8X4), lhsT_scale=plane[:, rows],
-                                    rhs=rhs.bitcast(FP8X4), rhs_scale=rhs_plane, start=True, stop=True)
+                nc.tensor.matmul_mx(
+                    bank[:, a, :], lhsT=codes[:, rows].bitcast(FP8X4), lhsT_scale=plane[:, rows],
+                    rhs=rhs.bitcast(FP8X4), rhs_scale=rhs_plane, start=True, stop=True,
+                )
 
         raw = {}
         for pair in range(2):
             for h in range(2):
-                raw[h, pair] = acc.tile([P, 2, HALF], F32, name=f"s{h}{pair}", tag="acc")
-                product_pair(raw[h, pair][:], d_codes, ds_plane, pair, x_codes[h][:], xs_plane[:, half_cols(h)])
+                raw[h, pair] = products.tile([P, 2, HALF], F32, name=f"raw{h}{pair}", tag="product")
+                product_pair(raw[h, pair][:], d_codes, d_plane, pair, x_codes[h][:], x_plane[:, half_cols(h)])
 
-        w1_codes = at(0, [P, S], U32, "w1_codes")
-        w1s_plane = at(2048, [P, S], U8, "w1s_plane")
-        gain = at(2560, [P, PACK], F32, "gain")
+        w1_codes = on_x_table(0, [P, S], U32, "w1_codes")
+        w1_plane = on_x_table(4 * S, [P, S], U8, "w1_plane")
+        gain = on_x_table(5 * S, [P, PACK], F32, "gain")
+        deal(w1_codes[:].bitcast(I32), w1_loaded[:])
+        deal(w1_plane[:], w1_scale_loaded[:])
+        settle(nc.sync, w1_plane)
+        nc.vector.tensor_scalar(gain[:], gn_t[:], GAIN, None, ALU.mult)
 
         score = [sb([P, S], F32, f"score{t}") for t in range(PACK)]
-        units = [(h, t) for h in range(2) for t in range(PACK)]
-        n = len(units)
-        direct = n - 2
-        xk = [sb([P, 2, HALF], F32, f"xk{v}") for v in range(n // 2)]
-        yk = [sb([P, 2, HALF], F32, f"yk{v}") for v in range(n // 2)]
-        g1 = [sb([P, HALF], F32, f"g1{u}") for u in range(n)]
-        nn = [sb([P, HALF], F32, f"nn{u}") for u in range(n)]
-        ee = [sb([P, HALF], F32, f"ee{u}") for u in range(n)]
-        rr = [sb([P, HALF], F32, f"rr{u}") for u in range(n)]
-        lin, den, sq = {}, {}, {}
-        z_rows = [sb([P, PACK, HALF], BF16, f"z_rows{h}") for h in range(2)]
-        z_in = [sb([P, HALF, PACK], BF16, f"z_in{h}") for h in range(2)]
-        z_codes = [sb([P, HALF], U32, f"z_codes{h}") for h in range(2)]
-        z_plane = [sb([P, HALF], U8, f"z_plane{h}") for h in range(2)]
-        hid = [at(8192 + 2048 * t, [P, S], F32, f"hid{t}") for t in range(PACK)]
+        lead_term = [sb([P, 2, HALF], F32, f"lead_term{v}") for v in range(len(UNITS) // 2)]
+        even_term = [sb([P, 2, HALF], F32, f"even_term{v}") for v in range(TURNED // 2)]
+        lead = [sb([P, HALF], F32, f"lead{u}") for u in range(len(UNITS))]
+        total_half = [sb([P, PACK, HALF], F32, f"total{h}") for h in range(2)]
+        total = [total_half[h][:, t, :] for h, t in UNITS]
+        odd_part = [sb([P, HALF], F32, f"odd_part{u}") for u in range(len(UNITS))]
+        inv_root = [sb([P, HALF], F32, f"inv_root{u}") for u in range(len(UNITS))]
+        factor = sb([P, PACK, HALF], F32, "factor")
+        forms, squared, spread = {}, {}, {}
 
-        def window(t, h, copy):
+        def fill_window(t, h, copy):
             copy(score[t][:, half_cols(h)], raw[h, t // 2][:, t % 2, :])
 
-        def scaled(dst, v, factor, count=2):
-            nc.scalar.activation(dst[v][:, :count, :], raw[v // 2, v % 2][:, :count, :], ACT.Copy, scale=factor)
+        def scale_raw(dst, v, scale):
+            nc.scalar.activation(dst[v][:], raw[v // 2, v % 2][:], ACT.Copy, scale=scale)
 
-        def add_turned(out, a, b):
-            nc.tensor.matmul(out, a, ident[:], start=True, stop=False, is_transpose=True)
-            nc.tensor.matmul(out, b, ident[:], start=False, stop=True, is_transpose=True)
+        def add_turned(out, first, second):
+            nc.tensor.matmul(out, first, ident[:], start=True, stop=False, is_transpose=True)
+            nc.tensor.matmul(out, second, ident[:], start=False, stop=True, is_transpose=True)
 
         def look_up(v):
             pair = (2 * v, 2 * v + 1)
             for u in pair:
-                h, t = units[u]
-                nc.vector.tensor_tensor(g1[u][:], score[t][:].indirect(half_list(n1_t, h)), xk[v][:, u % 2, :], ALU.subtract)
+                h, t = UNITS[u]
+                picked = score[t][:].indirect(entries(n1_t, h * HALF, HALF))
+                nc.vector.tensor_tensor(lead[u][:], picked, lead_term[v][:, u % 2, :], ALU.subtract)
             for u in pair:
-                h, t = units[u]
-                nc.vector.tensor_tensor(nn[u][:], score[t][:].indirect(half_list(n2_t, h)), g1[u][:], ALU.add)
+                h, t = UNITS[u]
+                picked = score[t][:].indirect(entries(n2_t, h * HALF, HALF))
+                nc.vector.tensor_tensor(total[u], picked, lead[u][:], ALU.add)
             for u in pair:
-                nc.vector.scalar_tensor_tensor(ee[u][:], g1[u][:], 2.0, nn[u][:], ALU.mult, ALU.subtract)
+                nc.vector.scalar_tensor_tensor(odd_part[u][:], lead[u][:], 2.0, total[u], ALU.mult, ALU.subtract)
 
-        def forms(u):
-            if u >= direct:
-                lin[u] = sb([P, 4, P], F32, f"lin_last{u}")
-                nc.vector.scalar_tensor_tensor(lin[u][:, 0:2, :].rearrange("p b c -> p (b c)"), raw[1, 1][:, u % 2, :], 8.0 / 15.0, nn[u][:], ALU.mult, ALU.add)
-                nc.vector.tensor_tensor(lin[u][:, 2:4, :].rearrange("p b c -> p (b c)"), xk[u // 2][:, u % 2, :], ee[u][:], ALU.add)
+        def make_forms(u):
+            h, t = UNITS[u]
+            if u >= TURNED:
+                forms[u] = sb([P, 4, P], F32, f"forms{u}")
+                own = raw[h, t // 2][:, t % 2, :]
+                nc.vector.scalar_tensor_tensor(flat(forms[u][:, 0:2, :]), own, EVEN, total[u], ALU.mult, ALU.add)
+                nc.vector.tensor_tensor(flat(forms[u][:, 2:4, :]), lead_term[u // 2][:, u % 2, :], odd_part[u][:], ALU.add)
                 return
-            lin[u] = turn.tile([P, 4, P], F32, name=f"lin{u}", tag="lin")
+            forms[u] = turns.tile([P, 4, P], F32, name=f"forms{u}", tag="forms")
             for b in range(2):
                 cols = slice(b * P, (b + 1) * P)
-                add_turned(lin[u][:, b, :], yk[u // 2][:, u % 2, cols], nn[u][:, cols])
+                add_turned(forms[u][:, b, :], even_term[u // 2][:, u % 2, cols], total[u][:, cols])
             for b in range(2):
                 cols = slice(b * P, (b + 1) * P)
-                add_turned(lin[u][:, 2 + b, :], xk[u // 2][:, u % 2, cols], ee[u][:, cols])
+                add_turned(forms[u][:, 2 + b, :], lead_term[u // 2][:, u % 2, cols], odd_part[u][:, cols])
 
-        def squares(u):
-            unit = 1.0 / (16.0 * math.sqrt(2.0))
-            sq[u] = ring.tile([P, 4, P], F32, name=f"sq{u}", tag="sq")
-            nc.scalar.activation(sq[u][:, 0:2, :], lin[u][:, 0:2, :], ACT.Square, scale=0.375 * unit)
-            nc.scalar.activation(sq[u][:, 2:4, :], lin[u][:, 2:4, :], ACT.Square, scale=unit)
-            if u >= direct:
-                den[u] = at(8192 + 1536, [P, HALF], F32, f"den_last{u}") if u == n - 1 else sb([P, HALF], F32, f"den_last{u}")
-                nc.vector.tensor_tensor(den[u][:], sq[u][:, 0:2, :].rearrange("p b c -> p (b c)"), sq[u][:, 2:4, :].rearrange("p b c -> p (b c)"), ALU.add)
+        def make_spread(u):
+            squared[u] = in_ring([P, 4, P], F32, f"squared{u}")
+            nc.scalar.activation(squared[u][:, 0:2, :], forms[u][:, 0:2, :], ACT.Square, scale=EVEN_SCALE)
+            nc.scalar.activation(squared[u][:, 2:4, :], forms[u][:, 2:4, :], ACT.Square, scale=ODD_SCALE)
+            if u >= TURNED:
+                spread[u] = sb([P, HALF], F32, f"spread{u}")
+                nc.vector.tensor_tensor(spread[u][:], flat(squared[u][:, 0:2, :]), flat(squared[u][:, 2:4, :]), ALU.add)
                 return
-            den[u] = turn.tile([P, HALF], F32, name=f"den{u}", tag="den")
+            spread[u] = turns.tile([P, HALF], F32, name=f"spread{u}", tag="spread")
             for b in range(2):
-                add_turned(den[u][:, b * P : (b + 1) * P], sq[u][:, b, :], sq[u][:, 2 + b, :])
+                add_turned(spread[u][:, b * P : (b + 1) * P], squared[u][:, b, :], squared[u][:, 2 + b, :])
 
-        def root(u):
-            nc.scalar.activation(rr[u][:], den[u][:], ACT.Abs_reciprocal_sqrt, bias=quarter)
+        def make_root(u):
+            nc.scalar.activation(inv_root[u][:], spread[u][:], ACT.Abs_reciprocal_sqrt, bias=quarter[:])
 
-        def weave(copy, dst, src):
-            copy(dst.rearrange("p (c i) t -> p c t i", i=4), src.rearrange("p t (c i) -> p c t i", i=4))
+        def make_factor(t):
+            nc.scalar.activation(factor[:, t, :], inv_root[t][:], ACT.Copy, scale=gain[:, t : t + 1])
 
-        def standardised(u):
-            h, t = units[u]
-            nc.vector.scalar_tensor_tensor(z_rows[h][:, t, :], nn[u][:], gain[:, t : t + 1], rr[u][:], ALU.mult, ALU.mult)
+        def tiles_view(ap, run):
+            return ap.rearrange("p t (c i) -> p c t i", i=run)
 
+        def woven_view(ap, run):
+            return ap.rearrange("p (c i) t -> p c t i", i=run)
+
+        def weave(dst, src):
+            nc.vector.tensor_copy(woven_view(dst, 4), tiles_view(src, 4))
+
+        scale_raw(lead_term, 0, LEAD)
+        for t in (0, 1):
+            fill_window(t, 0, nc.scalar.copy)
+            fill_window(t, 1, nc.vector.tensor_copy)
+        scale_raw(even_term, 0, EVEN)
+        for t in (2, 3):
+            fill_window(t, 0, nc.scalar.copy)
+            fill_window(t, 1, nc.scalar.copy)
+        for v in range(1, len(UNITS) // 2):
+            scale_raw(lead_term, v, LEAD)
+        for v in range(len(UNITS) // 2):
+            look_up(v)
+
+        make_forms(0)
+        for k in range(len(UNITS) + 1):
+            if k % 2 == 1 and k + 1 < TURNED:
+                scale_raw(even_term, (k + 1) // 2, EVEN)
+            if k + 1 < len(UNITS):
+                make_forms(k + 1)
+            if k < len(UNITS):
+                make_spread(k)
+            if k >= 1:
+                make_root(k - 1)
+            if 2 <= k < PACK + 2:
+                make_factor(k - 2)
+        warm_gate = sb([P, 1], F32, "warm_gate")
+        nc.scalar.activation(warm_gate[:], inv_root[-1][:, 0:1], ACT.Sigmoid)
+
+        z_codes = [sb([P, HALF], U32, f"z_codes{h}") for h in range(2)]
+        z_plane = [sb([P, HALF], U8, f"z_plane{h}") for h in range(2)]
+        quarters = (slice(0, P), slice(P, HALF))
         sums = {}
-        late = []
 
-        def values(h):
-            pieces = [slice(0, HALF)] if h == 0 else [slice(0, P), slice(P, HALF)]
+        def second_product(h, z_woven, pieces):
             for cols in pieces:
-                weave(nc.vector.tensor_copy, z_in[h][:, cols, :], z_rows[h][:, :, cols])
-            for cols in pieces:
-                nc.vector.quantize_mx(z_codes[h][:, cols].bitcast(FP8X4), z_plane[h][:, cols], z_in[h][:, cols, :].rearrange("p j t -> p (j t)"))
+                nc.vector.quantize_mx(z_codes[h][:, cols].bitcast(FP8X4), z_plane[h][:, cols], flat(z_woven[:, cols, :]))
             for pair in range(2):
-                sums[h, pair] = acc.tile([P, 2, HALF], F32, name=f"h{h}{pair}", tag="acc")
+                sums[h, pair] = products.tile([P, 2, HALF], F32, name=f"sums{h}{pair}", tag="product")
             for cols in pieces:
                 for pair in range(2):
-                    product_pair(sums[h, pair][:, :, cols], w1_codes, w1s_plane, pair, z_codes[h][:, cols], z_plane[h][:, cols])
-            for t in range(PACK):
-                copy = nc.scalar.copy if h == 0 and t < 2 else nc.vector.tensor_copy
-                late.append((copy, t, h))
+                    product_pair(sums[h, pair][:, :, cols], w1_codes, w1_plane, pair, z_codes[h][:, cols], z_plane[h][:, cols])
 
-        deal(w1_codes[:].bitcast(I32), w1_raw[:])
-        deal(w1s_plane[:], w1s_raw[:])
-        settle(nc.sync, w1s_plane)
-        nc.vector.tensor_scalar(gain[:], gn_t[:], -5.0 / 256.0, None, ALU.mult)
-        scaled(xk, 0, 2.2)
-        for t in (0, 1):
-            window(t, 0, nc.scalar.copy)
-            window(t, 1, nc.vector.tensor_copy)
-        scaled(yk, 0, 8.0 / 15.0)
-        for t in (2, 3):
-            window(t, 0, nc.scalar.copy)
-            window(t, 1, nc.scalar.copy)
-        for v in (1, 2, 3):
-            scaled(xk, v, 2.2)
-        for v in range(n // 2):
-            look_up(v)
-        forms(0)
-        for k in range(n + 1):
-            if k < n:
-                if k % 2 == 1 and k + 1 < direct:
-                    scaled(yk, (k + 1) // 2, 8.0 / 15.0, min(2, direct - k - 1))
-                if k + 1 < n:
-                    forms(k + 1)
-                squares(k)
-            if k >= 1:
-                root(k - 1)
-                standardised(k - 1)
-                if k % PACK == 0:
-                    values(k // PACK - 1)
-        warm_gate = sb([P, 1], F32, "warm_gate")
-        nc.scalar.activation(warm_gate[:], rr[n - 1][:, 0:1], ACT.Sigmoid)
-        for copy, t, h in late:
-            copy(hid[t][:, half_cols(h)], sums[h, t // 2][:, t % 2, :])
+        z_first = in_ring([P, HALF, PACK], BF16, "z_first")
+        for cols in quarters:
+            nc.vector.tensor_tensor(
+                woven_view(z_first[:, cols, :], 2), tiles_view(total_half[0][:, :, cols], 2), tiles_view(factor[:, :, cols], 2), ALU.mult
+            )
+        second_product(0, z_first, [slice(0, HALF)])
+        z_rows = in_ring([P, PACK, HALF], BF16, "z_rows")
+        z_second = sb([P, HALF, PACK], BF16, "z_second")
+        for t in range(PACK):
+            u = PACK + t
+            nc.vector.scalar_tensor_tensor(z_rows[:, t, :], total[u], gain[:, t : t + 1], inv_root[u][:], ALU.mult, ALU.mult)
+        for cols in quarters:
+            weave(z_second[:, cols, :], z_rows[:, :, cols])
+        second_product(1, z_second, quarters)
+
+        hidden = [sb([P, S], F32, f"hidden{t}") for t in range(PACK)]
+        for h, copy in ((0, nc.scalar.copy), (1, nc.vector.tensor_copy)):
+            for t in range(PACK):
+                copy(hidden[t][:, half_cols(h)], sums[h, t // 2][:, t % 2, :])
 
         out_rows = out_0.rearrange("(p t) j -> p t j", t=PACK)
-        o_codes = sb([P, S], U32, "o_codes")
-        o_plane = sb([P, S], U8, "o_plane")
-        for lo, width in ((0, 256), (256, 128), (384, 128)):
+        out_codes = sb([P, S], U32, "out_codes")
+        out_plane = sb([P, S], U8, "out_plane")
+        for lo, width in OUT_PIECES:
             cols = slice(lo, lo + width)
-            res = sb([P, PACK, width], F32, f"res{lo}")
-            o_in = sb([P, width, PACK], BF16, f"o_in{lo}")
+            result = sb([P, PACK, width], F32, f"result{lo}")
+            out_woven = sb([P, width, PACK], BF16, f"out_woven{lo}")
             for pair in range(2):
-                gate = sb([P, 2, width], F32, f"gate{lo}{pair}")
+                gate = sb([P, 2, width], F32, f"gate{lo}_{pair}")
                 for a in range(2):
-                    nc.scalar.activation(gate[:, a, :], hid[2 * pair + a][:].indirect(n3_t[:, lo // 16 : (lo + width) // 16]), ACT.Sigmoid)
+                    nc.scalar.activation(gate[:, a, :], hidden[2 * pair + a][:].indirect(entries(n3_t, lo, width)), ACT.Sigmoid)
                 own = sums[lo // HALF, pair][:, :, lo % HALF : lo % HALF + width]
-                nc.vector.tensor_tensor(res[:, 2 * pair : 2 * pair + 2, :], own, gate[:], ALU.mult)
-            nc.sync.dma_start(out_rows[:, :, cols], res[:])
-            weave(nc.vector.tensor_copy, o_in[:], res[:])
-            nc.vector.quantize_mx(o_codes[:, cols].bitcast(FP8X4), o_plane[:, cols], o_in[:].rearrange("p j t -> p (j t)"))
-            nc.sync.dma_start(words_of(out_1)[:, cols], o_codes[:, cols].bitcast(I32))
-        for q in range(4):
+                nc.vector.tensor_tensor(result[:, 2 * pair : 2 * pair + 2, :], own, gate[:], ALU.mult)
+            nc.sync.dma_start(out_rows[:, :, cols], result[:])
+            weave(out_woven[:], result[:])
+            nc.vector.quantize_mx(out_codes[:, cols].bitcast(FP8X4), out_plane[:, cols], flat(out_woven[:]))
+            nc.sync.dma_start(words_of(out_1)[:, cols], out_codes[:, cols].bitcast(I32))
+        for q in range(P // QUAD):
             queue = nc.scalar if q % 2 else nc.sync
-            queue.dma_start(out_2[0, 4 * q : 4 * q + 4, :].bitcast(I32), o_plane[32 * q : 32 * q + 4, :].bitcast(I32))
+            rows = out_plane[QUAD * q : QUAD * q + PACK, :]
+            queue.dma_start(out_2[0, PACK * q : PACK * q + PACK, :].bitcast(I32), rows.bitcast(I32))

import math
from contextlib import ExitStack

import concourse.mybir as mybir
from concourse.masks import make_identity

F32 = mybir.dt.float32
BF16 = mybir.dt.bfloat16
I32 = mybir.dt.int32
U32 = mybir.dt.uint32
U16 = mybir.dt.uint16
U8 = mybir.dt.uint8
FP8X4 = mybir.dt.float8_e4m3fn_x4
ALU = mybir.AluOpType
ACT = mybir.ActivationFunctionType

P = 128
PACK = 4
BLOCK_PARTS = 8
QUAD = 32
GROUP = 16
TABLE = 2048
S = 512
HALF = S // 2
UNITS = [(h, t) for h in range(2) for t in range(PACK)]
TURNED = len(UNITS) - 2
OUT_PIECES = ((0, 256), (256, 128), (384, 128))

LEAD = 11.0 / 5.0
EVEN = 8.0 / 15.0
ODD_SCALE = 1.0 / math.sqrt(512.0)
EVEN_SCALE = 0.375 * ODD_SCALE
GAIN = -5.0 / 256.0

FLOPS = 2 * 2 * 512 * 512 * 512


def tile_picked_keystdgate_none_po_kernel(
    tc, x_words, x_scales, d_words, d_scales, gn, w1_words, w1_scales, offs, kidx, n1, n2, n3, out_0, out_1, out_2
):
    nc = tc.nc
    with ExitStack() as ctx:
        lists = ctx.enter_context(tc.tile_pool(name="lists", bufs=1))
        keep = ctx.enter_context(tc.tile_pool(name="keep", bufs=1))
        reused = ctx.enter_context(tc.tile_pool(name="reused", bufs=1))
        ring = ctx.enter_context(tc.tile_pool(name="ring", bufs=2))
        products = ctx.enter_context(tc.psum_pool(name="products", bufs=4))
        turns = ctx.enter_context(tc.psum_pool(name="turns", bufs=2))

        def sb(shape, dtype, name):
            return keep.tile(shape, dtype, name=name, align_bytes=64)

        def on_x_table(offset, shape, dtype, name):
            return reused.tile(shape, dtype, name=name, align_bytes=64, offset=offset)

        def in_ring(shape, dtype, name):
            return ring.tile(shape, dtype, name=name, tag="ring", align_bytes=64)

        def words_of(dram):
            return dram[0].rearrange("p n t -> p (n t)").bitcast(I32)

        def half_cols(h):
            return slice(h * HALF, (h + 1) * HALF)

        def entries(list_tile, lo, count):
            return list_tile[:, lo // GROUP : (lo + count) // GROUP]

        def flat(ap):
            return ap.rearrange("p b c -> p (b c)")

        kidx_t = lists.tile([P, S // GROUP], U16, name="kidx_t")
        offs_t = lists.tile([P, S // GROUP], U16, name="offs_t")
        n1_t = lists.tile([P, S // GROUP], U16, name="n1_t")
        n2_t = lists.tile([P, S // GROUP], U16, name="n2_t")
        n3_t = lists.tile([P, S // GROUP], U16, name="n3_t")

        d_table = sb([P, TABLE], I32, "d_table")
        x_table = on_x_table(0, [P, TABLE], I32, "x_table")
        d_scale_table = sb([P, TABLE], U8, "d_scale_table")
        x_scale_table = sb([P, TABLE], U8, "x_scale_table")
        w1_loaded = sb([P, S], I32, "w1_loaded")
        w1_scale_loaded = sb([P, S], U8, "w1_scale_loaded")
        gn_t = sb([P, PACK], F32, "gn_t")
        quarter = sb([P, 1], F32, "quarter")
        warm_root = sb([P, 1], F32, "warm_root")

        nc.vector.memset(d_scale_table[:].bitcast(I32), 0)
        nc.vector.memset(x_scale_table[:, : TABLE // 2].bitcast(I32), 0)
        nc.gpsimd.memset(x_scale_table[:, TABLE // 2 :].bitcast(I32), 0)
        nc.vector.memset(quarter[:], 0.25)
        nc.scalar.activation(warm_root[:], quarter[:], ACT.Abs_reciprocal_sqrt, bias=quarter[:])

        for list_tile, dram in ((kidx_t, kidx), (offs_t, offs), (n1_t, n1), (n2_t, n2)):
            nc.sync.dma_start(list_tile[:], dram)
        nc.sync.dma_start(gn_t[:], gn.rearrange("(p t) o -> p (t o)", t=PACK))
        nc.sync.dma_start(d_scale_table[0:P:BLOCK_PARTS, :].bitcast(I32), d_scales[0].bitcast(I32))
        nc.sync.dma_start(x_scale_table[0:P:BLOCK_PARTS, :].bitcast(I32), x_scales[0].bitcast(I32))
        nc.sync.dma_start(d_table[:], words_of(d_words))
        nc.sync.dma_start(x_table[:], words_of(x_words))
        nc.sync.dma_start(w1_loaded[:], words_of(w1_words))
        nc.sync.dma_start(n3_t[:], n3)
        nc.gpsimd.memset(w1_scale_loaded[:].bitcast(I32), 0)
        nc.sync.dma_start(w1_scale_loaded[0:P:BLOCK_PARTS, :].bitcast(I32), w1_scales[0].bitcast(I32))
        ident = sb([P, P], F32, "ident")
        make_identity(nc, ident[:])

        def deal(dst, src):
            nc.vector.tensor_copy(dst.rearrange("p (t m) -> p m t", t=PACK), src.rearrange("p (m t) -> p m t", t=PACK))

        def settle(queue, plane):
            for i in range(1, PACK):
                queue.dma_start(plane[i:P:QUAD, :].bitcast(I32), plane[BLOCK_PARTS * i : P : QUAD, :].bitcast(I32))

        d_scale_picked = sb([P, S], U8, "d_scale_picked")
        x_scale_picked = sb([P, S], U8, "x_scale_picked")
        planes = sb([P, 2 * S], U8, "planes")
        d_plane = planes[:, :S]
        x_plane = planes[:, S:]
        nc.vector.tensor_copy(d_scale_picked[:], d_scale_table[:].indirect(kidx_t[:]))
        nc.vector.tensor_copy(x_scale_picked[:], x_scale_table[:].indirect(offs_t[:]))
        deal(d_plane, d_scale_picked[:])
        nc.vector.tensor_copy(x_plane.bitcast(I32), x_scale_picked[:].bitcast(I32))
        settle(nc.scalar, planes)

        d_picked = sb([P, S], U32, "d_picked")
        d_codes = sb([P, S], U32, "d_codes")
        nc.vector.tensor_copy(d_picked[:], d_table[:].bitcast(U32).indirect(kidx_t[:]))
        deal(d_codes[:].bitcast(I32), d_picked[:].bitcast(I32))
        x_codes = [sb([P, HALF], U32, f"x_codes{h}") for h in range(2)]
        for h in range(2):
            nc.vector.tensor_copy(x_codes[h][:], x_table[:].bitcast(U32).indirect(entries(offs_t, h * HALF, HALF)))

        def product_pair(bank, codes, plane, pair, rhs, rhs_plane):
            for a in range(2):
                rows = slice((2 * pair + a) * P, (2 * pair + a + 1) * P)
                nc.tensor.matmul_mx(
                    bank[:, a, :], lhsT=codes[:, rows].bitcast(FP8X4), lhsT_scale=plane[:, rows],
                    rhs=rhs.bitcast(FP8X4), rhs_scale=rhs_plane, start=True, stop=True,
                )

        raw = {}
        for pair in range(2):
            for h in range(2):
                raw[h, pair] = products.tile([P, 2, HALF], F32, name=f"raw{h}{pair}", tag="product")
                product_pair(raw[h, pair][:], d_codes, d_plane, pair, x_codes[h][:], x_plane[:, half_cols(h)])

        w1_codes = on_x_table(0, [P, S], U32, "w1_codes")
        w1_plane = on_x_table(4 * S, [P, S], U8, "w1_plane")
        gain = on_x_table(5 * S, [P, PACK], F32, "gain")
        deal(w1_codes[:].bitcast(I32), w1_loaded[:])
        deal(w1_plane[:], w1_scale_loaded[:])
        settle(nc.sync, w1_plane)
        nc.vector.tensor_scalar(gain[:], gn_t[:], GAIN, None, ALU.mult)

        score = [sb([P, S], F32, f"score{t}") for t in range(PACK)]
        lead_term = [sb([P, 2, HALF], F32, f"lead_term{v}") for v in range(len(UNITS) // 2)]
        even_term = [sb([P, 2, HALF], F32, f"even_term{v}") for v in range(TURNED // 2)]
        lead = [sb([P, HALF], F32, f"lead{u}") for u in range(len(UNITS))]
        total_half = [sb([P, PACK, HALF], F32, f"total{h}") for h in range(2)]
        total = [total_half[h][:, t, :] for h, t in UNITS]
        odd_part = [sb([P, HALF], F32, f"odd_part{u}") for u in range(len(UNITS))]
        inv_root = [sb([P, HALF], F32, f"inv_root{u}") for u in range(len(UNITS))]
        factor = sb([P, PACK, HALF], F32, "factor")
        forms, squared, spread = {}, {}, {}

        def fill_window(t, h, copy):
            copy(score[t][:, half_cols(h)], raw[h, t // 2][:, t % 2, :])

        def scale_raw(dst, v, scale):
            nc.scalar.activation(dst[v][:], raw[v // 2, v % 2][:], ACT.Copy, scale=scale)

        def add_turned(out, first, second):
            nc.tensor.matmul(out, first, ident[:], start=True, stop=False, is_transpose=True)
            nc.tensor.matmul(out, second, ident[:], start=False, stop=True, is_transpose=True)

        def look_up(v):
            pair = (2 * v, 2 * v + 1)
            for u in pair:
                h, t = UNITS[u]
                picked = score[t][:].indirect(entries(n1_t, h * HALF, HALF))
                nc.vector.tensor_tensor(lead[u][:], picked, lead_term[v][:, u % 2, :], ALU.subtract)
            for u in pair:
                h, t = UNITS[u]
                picked = score[t][:].indirect(entries(n2_t, h * HALF, HALF))
                nc.vector.tensor_tensor(total[u], picked, lead[u][:], ALU.add)
            for u in pair:
                nc.vector.scalar_tensor_tensor(odd_part[u][:], lead[u][:], 2.0, total[u], ALU.mult, ALU.subtract)

        def make_forms(u):
            h, t = UNITS[u]
            if u >= TURNED:
                forms[u] = sb([P, 4, P], F32, f"forms{u}")
                own = raw[h, t // 2][:, t % 2, :]
                nc.vector.scalar_tensor_tensor(flat(forms[u][:, 0:2, :]), own, EVEN, total[u], ALU.mult, ALU.add)
                nc.vector.tensor_tensor(flat(forms[u][:, 2:4, :]), lead_term[u // 2][:, u % 2, :], odd_part[u][:], ALU.add)
                return
            forms[u] = turns.tile([P, 4, P], F32, name=f"forms{u}", tag="forms")
            for b in range(2):
                cols = slice(b * P, (b + 1) * P)
                add_turned(forms[u][:, b, :], even_term[u // 2][:, u % 2, cols], total[u][:, cols])
            for b in range(2):
                cols = slice(b * P, (b + 1) * P)
                add_turned(forms[u][:, 2 + b, :], lead_term[u // 2][:, u % 2, cols], odd_part[u][:, cols])

        def make_spread(u):
            squared[u] = in_ring([P, 4, P], F32, f"squared{u}")
            nc.scalar.activation(squared[u][:, 0:2, :], forms[u][:, 0:2, :], ACT.Square, scale=EVEN_SCALE)
            nc.scalar.activation(squared[u][:, 2:4, :], forms[u][:, 2:4, :], ACT.Square, scale=ODD_SCALE)
            if u >= TURNED:
                spread[u] = sb([P, HALF], F32, f"spread{u}")
                nc.vector.tensor_tensor(spread[u][:], flat(squared[u][:, 0:2, :]), flat(squared[u][:, 2:4, :]), ALU.add)
                return
            spread[u] = turns.tile([P, HALF], F32, name=f"spread{u}", tag="spread")
            for b in range(2):
                add_turned(spread[u][:, b * P : (b + 1) * P], squared[u][:, b, :], squared[u][:, 2 + b, :])

        def make_root(u):
            nc.scalar.activation(inv_root[u][:], spread[u][:], ACT.Abs_reciprocal_sqrt, bias=quarter[:])

        def make_factor(t):
            nc.scalar.activation(factor[:, t, :], inv_root[t][:], ACT.Copy, scale=gain[:, t : t + 1])

        def tiles_view(ap, run):
            return ap.rearrange("p t (c i) -> p c t i", i=run)

        def woven_view(ap, run):
            return ap.rearrange("p (c i) t -> p c t i", i=run)

        def weave(dst, src):
            nc.vector.tensor_copy(woven_view(dst, 4), tiles_view(src, 4))

        scale_raw(lead_term, 0, LEAD)
        for t in (0, 1):
            fill_window(t, 0, nc.scalar.copy)
            fill_window(t, 1, nc.vector.tensor_copy)
        scale_raw(even_term, 0, EVEN)
        for t in (2, 3):
            fill_window(t, 0, nc.scalar.copy)
            fill_window(t, 1, nc.scalar.copy)
        for v in range(1, len(UNITS) // 2):
            scale_raw(lead_term, v, LEAD)
        for v in range(len(UNITS) // 2):
            look_up(v)

        make_forms(0)
        for k in range(len(UNITS) + 1):
            if k % 2 == 1 and k + 1 < TURNED:
                scale_raw(even_term, (k + 1) // 2, EVEN)
            if k + 1 < len(UNITS):
                make_forms(k + 1)
            if k < len(UNITS):
                make_spread(k)
            if k >= 1:
                make_root(k - 1)
            if 2 <= k < PACK + 2:
                make_factor(k - 2)
        warm_gate = sb([P, 1], F32, "warm_gate")
        nc.scalar.activation(warm_gate[:], inv_root[-1][:, 0:1], ACT.Sigmoid)

        z_codes = [sb([P, HALF], U32, f"z_codes{h}") for h in range(2)]
        z_plane = [sb([P, HALF], U8, f"z_plane{h}") for h in range(2)]
        quarters = (slice(0, P), slice(P, HALF))
        sums = {}

        def second_product(h, z_woven, pieces):
            for cols in pieces:
                nc.vector.quantize_mx(z_codes[h][:, cols].bitcast(FP8X4), z_plane[h][:, cols], flat(z_woven[:, cols, :]))
            for pair in range(2):
                sums[h, pair] = products.tile([P, 2, HALF], F32, name=f"sums{h}{pair}", tag="product")
            for cols in pieces:
                for pair in range(2):
                    product_pair(sums[h, pair][:, :, cols], w1_codes, w1_plane, pair, z_codes[h][:, cols], z_plane[h][:, cols])

        z_first = in_ring([P, HALF, PACK], BF16, "z_first")
        for cols in quarters:
            nc.vector.tensor_tensor(
                woven_view(z_first[:, cols, :], 2), tiles_view(total_half[0][:, :, cols], 2), tiles_view(factor[:, :, cols], 2), ALU.mult
            )
        second_product(0, z_first, [slice(0, HALF)])
        z_rows = in_ring([P, PACK, HALF], BF16, "z_rows")
        z_second = sb([P, HALF, PACK], BF16, "z_second")
        for t in range(PACK):
            u = PACK + t
            nc.vector.scalar_tensor_tensor(z_rows[:, t, :], total[u], gain[:, t : t + 1], inv_root[u][:], ALU.mult, ALU.mult)
        for cols in quarters:
            weave(z_second[:, cols, :], z_rows[:, :, cols])
        second_product(1, z_second, quarters)

        hidden = [sb([P, S], F32, f"hidden{t}") for t in range(PACK)]
        for h, copy in ((0, nc.scalar.copy), (1, nc.vector.tensor_copy)):
            for t in range(PACK):
                copy(hidden[t][:, half_cols(h)], sums[h, t // 2][:, t % 2, :])

        out_rows = out_0.rearrange("(p t) j -> p t j", t=PACK)
        out_codes = sb([P, S], U32, "out_codes")
        out_plane = sb([P, S], U8, "out_plane")
        for lo, width in OUT_PIECES:
            cols = slice(lo, lo + width)
            result = sb([P, PACK, width], F32, f"result{lo}")
            out_woven = sb([P, width, PACK], BF16, f"out_woven{lo}")
            for pair in range(2):
                gate = sb([P, 2, width], F32, f"gate{lo}_{pair}")
                for a in range(2):
                    nc.scalar.activation(gate[:, a, :], hidden[2 * pair + a][:].indirect(entries(n3_t, lo, width)), ACT.Sigmoid)
                own = sums[lo // HALF, pair][:, :, lo % HALF : lo % HALF + width]
                nc.vector.tensor_tensor(result[:, 2 * pair : 2 * pair + 2, :], own, gate[:], ALU.mult)
            nc.sync.dma_start(out_rows[:, :, cols], result[:])
            weave(out_woven[:], result[:])
            nc.vector.quantize_mx(out_codes[:, cols].bitcast(FP8X4), out_plane[:, cols], flat(out_woven[:]))
            nc.sync.dma_start(words_of(out_1)[:, cols], out_codes[:, cols].bitcast(I32))
        for q in range(P // QUAD):
            queue = nc.scalar if q % 2 else nc.sync
            rows = out_plane[QUAD * q : QUAD * q + PACK, :]
            queue.dma_start(out_2[0, PACK * q : PACK * q + PACK, :].bitcast(I32), rows.bitcast(I32))
